import numpy as np
import ml_dtypes


def mxq(x, axis, fmt="e4m3"):
    dtype, down = {"e4m3": (ml_dtypes.float8_e4m3fn, 7), "e5m2": (ml_dtypes.float8_e5m2, 14)}[fmt]
    v = np.moveaxis(np.asarray(x, np.float32).astype(ml_dtypes.bfloat16).astype(np.float64), axis, -1)
    blocks = v.reshape(v.shape[:-1] + (-1, 32))
    amax = np.abs(blocks).max(-1, keepdims=True)
    byte = np.maximum(np.where(amax > 0, np.frexp(amax)[1] - 1 + 127, 0) - down, 1)
    scale = np.exp2(byte - 127.0)
    codes = (blocks / scale).astype(np.float32).astype(dtype).astype(np.float64)
    return np.moveaxis((codes * scale).reshape(v.shape), -1, axis)


WIDE = False


def mx_kscale(k):
    if not WIDE:
        return np.ones(k)
    levels = np.array([30, -30])
    if k % 512:
        return np.exp2(np.random.permutation(np.resize(levels, k // 32))).repeat(32)
    a = np.empty((k // 512, 16))
    for p in range(k // 512):
        a[p, :8] = np.random.permutation(np.resize(levels, 8))
        for g in range(8):
            far = levels[np.abs(levels - a[p, g]) >= 10]
            a[p, g + 8] = far[np.random.randint(len(far))]
    return np.exp2(a.ravel()).repeat(32)


def f64(x):
    return np.asarray(x).astype(np.float64)


def striped(idx):
    return np.tile(np.asarray(idx).reshape(-1, 16).T, (8, 1)).astype(np.uint16)


def unstriped(offs):
    return offs[:16].T.reshape(-1).astype(np.int64)


E2M1 = np.array([0.0, 0.5, 1.0, 1.5, 2.0, 3.0, 4.0, 6.0, -0.0, -0.5, -1.0, -1.5, -2.0, -3.0, -4.0, -6.0])


def pack_weight(w, fmt):
    k, n = w.shape
    w = f64(np.asarray(w, np.float32).astype(ml_dtypes.bfloat16)).reshape(k // 32, 32, n)
    amax = np.abs(w).max(1)
    if fmt in ("e4m3", "e5m2"):
        byte = np.frexp(amax)[1] - 1 + 127 - (7 if fmt == "e4m3" else 14)
    else:
        mant, ex = np.frexp(amax / 6.0)
        byte = np.where(mant > 0.5, ex, ex - 1) + 127
    byte = np.clip(np.where(amax > 0, byte, 1), 1, 254)
    scaled = (w * np.exp2(127.0 - byte)[:, None, :]).reshape(k, n).astype(np.float32)
    by_word = np.ascontiguousarray(scaled.reshape(k // 512, 128, 4, n).transpose(0, 1, 3, 2))
    if fmt in ("e4m3", "e5m2"):
        words = by_word.astype(ml_dtypes.float8_e4m3fn if fmt == "e4m3" else ml_dtypes.float8_e5m2).view(np.uint8)
    else:
        c = by_word.astype(ml_dtypes.float4_e2m1fn).view(np.uint8) & 0xF
        words = (c[..., 0::2] | (c[..., 1::2] << 4)).reshape(k // 512, 128, 2 * n)
    return np.ascontiguousarray(words), np.ascontiguousarray(byte.astype(np.uint8).reshape(k // 512, 16, n))


def unpack_weight(words, scales, fmt):
    g, _, n = scales.shape
    words = np.ascontiguousarray(words).reshape(g, 128, n, -1)
    if fmt in ("e4m3", "e5m2"):
        vals = words.view(ml_dtypes.float8_e4m3fn if fmt == "e4m3" else ml_dtypes.float8_e5m2).astype(np.float64)
    else:
        nib = np.empty((g, 128, n, 4), np.uint8)
        nib[..., 0::2] = words & 0xF
        nib[..., 1::2] = words >> 4
        vals = E2M1[nib]
    vals = vals * np.repeat(np.exp2(scales.astype(np.float64) - 127.0), 8, axis=1)[..., None]
    return vals.transpose(0, 1, 3, 2).reshape(g * 512, n)


K, T, J, N, L = 1024, 1024, 256, 256, 512


def setup_inputs():
    n = np.random.standard_normal
    idx = np.random.permutation(T)[:J]
    fk = mx_kscale(K)
    fl = mx_kscale(L)
    xtp = pack_weight(n((K, T)) * np.random.uniform(0.4, 1.6, (1, T)) / fk[:, None], "e4m3")
    wap = pack_weight(n((K, N)) * 1 / np.sqrt(K) * fk[:, None], "e5m2")
    wbp = pack_weight(n((L, N)) * 1 / np.sqrt(L) * fl[:, None], "e5m2")
    return {
        "xt_words": xtp[0],
        "xt_scales": xtp[1],
        "wa_words": wap[0],
        "wa_scales": wap[1],
        "sx": (n((L, J)) * np.random.uniform(0.4, 1.6, (1, J)) / fl[:, None]).astype(np.float32),
        "wb_words": wbp[0],
        "wb_scales": wbp[1],
        "bi": (np.random.uniform(-0.6, 0.6, (1, N))).astype(np.float32),
        "rs": (1.0 * n((J, N))).astype(np.float32),
        "offs": striped(idx),
    }


def reference(xt_words, xt_scales, wa_words, wa_scales, sx, wb_words, wb_scales, bi, rs, offs):
    idx = unstriped(offs)
    xtu = unpack_weight(xt_words, xt_scales, "e4m3")
    wau = unpack_weight(wa_words, wa_scales, "e5m2")
    wbu = unpack_weight(wb_words, wb_scales, "e5m2")
    xtidxg = xtu[:, idx]
    a = xtidxg.T @ wau
    sxq = mxq(f64(sx), 0, "e5m2")
    b0 = sxq.T @ wbu
    b2 = b0 + f64(bi)
    d = a - b2
    y = d / (np.max(np.abs(d), axis=1, keepdims=True) + 0.2) + 0.3 * f64(rs)
    return y

@@ -1,0 +1,158 @@
+from contextlib import ExitStack
+
+import concourse.mybir as mybir
+from concourse.masks import make_identity
+
+K, T, J, N, L = 1024, 1024, 256, 256, 512
+FLOPS = 2 * J * N * (K + L)
+
+F32 = mybir.dt.float32
+BF16 = mybir.dt.bfloat16
+I32 = mybir.dt.int32
+U32 = mybir.dt.uint32
+U16 = mybir.dt.uint16
+U8 = mybir.dt.uint8
+E4M3 = mybir.dt.float8_e4m3fn_x4
+E5M2 = mybir.dt.float8_e5m2_x4
+ALU = mybir.AluOpType
+ACT = mybir.ActivationFunctionType
+
+P = 128
+PACK = 4
+PASSES = K // (P * PACK)
+QUADS = 4
+ROWS = 4
+JT = J // P
+
+
+def tile_list_rows_owninput_gapoverpeak_kernel(
+    tc, xt_words, xt_scales, wa_words, wa_scales, sx, wb_words, wb_scales, bi, rs, offs, out
+):
+    nc = tc.nc
+    with ExitStack() as ctx:
+        sb = ctx.enter_context(tc.tile_pool(name="sb", bufs=1))
+        ps = ctx.enter_context(tc.psum_pool(name="ps", bufs=1))
+
+        offsets = sb.tile([P, J // 16], U16, name="offsets")
+        xs = sb.tile([P, PASSES * T], U8, name="xs", tag="xs_then_wa", align_bytes=64)
+        ws = sb.tile([P, (PASSES + 1) * N], U8, name="ws", align_bytes=64)
+        xw = [sb.tile([P, T], I32, name="xw%d" % z, align_bytes=64) for z in range(PASSES)]
+        wbw = sb.tile([P, N], I32, name="wbw", align_bytes=64)
+        sx_raw = sb.tile([P, PACK, J], F32, name="sx_raw", tag="sx_then_rs", align_bytes=64)
+        bi_col = sb.tile([P, 2], F32, name="bi_col")
+        ident = sb.tile([P, P], F32, name="ident", align_bytes=64)
+
+        nc.vector.memset(xs[:].bitcast(I32), 0)
+        nc.vector.memset(ws[:].bitcast(I32), 0)
+
+        def scale_rows(queue, plane, first_word, src, q):
+            passes = src.shape[0]
+            words = src.shape[2] // 4
+            dst = plane[32 * q : 32 * q + ROWS, :].bitcast(I32)[:, first_word : first_word + passes * words]
+            queue.dma_start(
+                out=dst.rearrange("r (z c) -> r z c", z=passes),
+                in_=src[:, ROWS * q : ROWS * (q + 1), :].bitcast(I32).rearrange("z r c -> r z c"),
+            )
+
+        def words_of(src, z):
+            return src[z].rearrange("p c t -> p (c t)").bitcast(I32)
+
+        nc.sync.dma_start(offsets[:], offs)
+        nc.scalar.dma_start(out=sx_raw[:], in_=sx.rearrange("(p t) j -> p t j", t=PACK))
+        nc.scalar.dma_start(out=wbw[:], in_=words_of(wb_words, 0))
+        for z in range(PASSES):
+            nc.gpsimd.dma_start(out=xw[z][:], in_=words_of(xt_words, z))
+        nc.gpsimd.dma_start(out=bi_col[:], in_=bi.rearrange("o (p c) -> (o p) c", c=2))
+        nc.vector.memset(ident[:], 0.0)
+        make_identity(nc, ident[:], nomemset=True)
+        for q in range(QUADS):
+            scale_rows(nc.sync, xs, 0, xt_scales, q)
+        for q in range(QUADS):
+            scale_rows(nc.sync, ws, 0, wa_scales, q)
+        for q in range(QUADS):
+            scale_rows(nc.sync, ws, PASSES * N // 4, wb_scales, q)
+
+        gs = sb.tile([P, PASSES * J], U8, name="gs", align_bytes=64)
+        for z in range(PASSES):
+            nc.vector.tensor_copy(gs[:, z * J : (z + 1) * J], xs[:, z * T : (z + 1) * T].indirect(offsets[:]))
+
+        waw = sb.tile([P, PASSES, N], I32, name="waw", tag="xs_then_wa", align_bytes=64)
+        nc.sync.dma_start(out=waw[:], in_=wa_words.rearrange("z p c t -> p z (c t)").bitcast(I32))
+
+        sx_bf = sb.tile([P, J, PACK], BF16, name="sx_bf", align_bytes=64)
+        nc.scalar.activation(
+            out=sx_bf[:].rearrange("p (c i) t -> p c t i", i=4),
+            in_=sx_raw[:].rearrange("p t (c i) -> p c t i", i=4),
+            func=ACT.Copy,
+            scale=-1.0,
+        )
+
+        rs_raw = sb.tile([P, JT, N], F32, name="rs_raw", tag="sx_then_rs", align_bytes=64)
+        nc.sync.dma_start(out=rs_raw[:], in_=rs.rearrange("(h p) n -> p h n", p=P))
+
+        bi_ps = ps.tile([P, 2, P], F32, name="bi_ps")
+        for c in range(2):
+            nc.tensor.transpose(bi_ps[:, c, :], bi_col[:, c : c + 1].to_broadcast([P, P]), ident[:])
+        bias = sb.tile([P, N], F32, name="bias")
+        nc.scalar.copy(out=bias[:].rearrange("q (p c) -> q p c", c=2), in_=bi_ps[:].rearrange("q c p -> q p c"))
+
+        gw = [sb.tile([P, J], U32, name="gw%d" % z, align_bytes=64) for z in range(PASSES)]
+        nc.vector.tensor_copy(gw[0][:], xw[0][:].bitcast(U32).indirect(offsets[:]))
+
+        sq = sb.tile([P, J], U32, name="sq", align_bytes=64)
+        sqs = sb.tile([P, J], U8, name="sqs", align_bytes=64)
+        nc.vector.quantize_mx(out=sq[:].bitcast(E5M2), scales=sqs[:], in_=sx_bf[:].rearrange("p j t -> p (j t)"))
+
+        nc.vector.tensor_copy(gw[1][:], xw[1][:].bitcast(U32).indirect(offsets[:]))
+
+        rs3 = sb.tile([P, JT, N], F32, name="rs3")
+        nc.scalar.activation(out=rs3[:], in_=rs_raw[:], func=ACT.Copy, scale=0.3)
+
+        acc = [ps.tile([P, N], F32, name="acc%d" % h) for h in range(JT)]
+
+        def mx_pass(h, step):
+            cols = slice(h * P, (h + 1) * P)
+            if step == 0:
+                nc.tensor.matmul_mx(
+                    out=acc[h][:],
+                    lhsT=sq[:, cols].bitcast(E5M2),
+                    lhsT_scale=sqs[:, cols],
+                    rhs=wbw[:].bitcast(E5M2),
+                    rhs_scale=ws[:, PASSES * N : (PASSES + 1) * N],
+                    start=True,
+                    stop=False,
+                )
+            else:
+                z = step - 1
+                nc.tensor.matmul_mx(
+                    out=acc[h][:],
+                    lhsT=gw[z][:, cols].bitcast(E4M3),
+                    lhsT_scale=gs[:, z * J + h * P : z * J + (h + 1) * P],
+                    rhs=waw[:, z, :].bitcast(E5M2),
+                    rhs_scale=ws[:, z * N : (z + 1) * N],
+                    start=False,
+                    stop=(step == 2),
+                )
+
+        for h in range(JT):
+            mx_pass(h, 0)
+        for h in range(JT):
+            mx_pass(h, 1)
+            mx_pass(h, 2)
+
+        for h in range(JT):
+            d = sb.tile([P, N], F32, name="d%d" % h)
+            peak = sb.tile([P, 1], F32, name="peak%d" % h)
+            den = sb.tile([P, 1], F32, name="den%d" % h)
+            inv = sb.tile([P, 1], F32, name="inv%d" % h)
+            y = sb.tile([P, N], F32, name="y%d" % h)
+            nc.vector.tensor_tensor(out=d[:], in0=acc[h][:], in1=bias[:], op=ALU.subtract)
+            nc.vector.tensor_reduce(
+                out=peak[:], in_=d[:], axis=mybir.AxisListType.X, op=ALU.max, apply_absolute_value=True
+            )
+            nc.vector.tensor_scalar(out=den[:], in0=peak[:], scalar1=0.2, scalar2=None, op0=ALU.add)
+            nc.vector.reciprocal(out=inv[:], in_=den[:])
+            nc.vector.scalar_tensor_tensor(
+                out=y[:], in0=d[:], scalar=inv[:], in1=rs3[:, h, :], op0=ALU.mult, op1=ALU.add
+            )
+            (nc.sync if h == 0 else nc.scalar).dma_start(out=out[h * P : (h + 1) * P, :], in_=y[:])

@@ -1,7 +1,6 @@
 from contextlib import ExitStack
 
 import concourse.mybir as mybir
-from concourse.masks import make_identity
 
 K, T, J, N, L = 1024, 1024, 256, 256, 512
 FLOPS = 2 * J * N * (K + L)
@@ -34,13 +33,13 @@ def tile_list_rows_owninput_gapoverpeak_kernel(
         ps = ctx.enter_context(tc.psum_pool(name="ps", bufs=1))
 
         offsets = sb.tile([P, J // 16], U16, name="offsets")
-        xs = sb.tile([P, PASSES * T], U8, name="xs", tag="xs_then_wa", align_bytes=64)
+        xs = sb.tile([P, PASSES * T], U8, name="xs", align_bytes=64)
         ws = sb.tile([P, (PASSES + 1) * N], U8, name="ws", align_bytes=64)
         xw = [sb.tile([P, T], I32, name="xw%d" % z, align_bytes=64) for z in range(PASSES)]
         wbw = sb.tile([P, N], I32, name="wbw", align_bytes=64)
         sx_raw = sb.tile([P, PACK, J], F32, name="sx_raw", tag="sx_then_rs", align_bytes=64)
-        bi_col = sb.tile([P, 2], F32, name="bi_col")
-        ident = sb.tile([P, P], F32, name="ident", align_bytes=64)
+        waw = sb.tile([P, PASSES, N], I32, name="waw", align_bytes=64)
+        bias = sb.tile([P, N], F32, name="bias")
 
         nc.vector.memset(xs[:].bitcast(I32), 0)
         nc.vector.memset(ws[:].bitcast(I32), 0)
@@ -62,9 +61,8 @@ def tile_list_rows_owninput_gapoverpeak_kernel(
         nc.scalar.dma_start(out=wbw[:], in_=words_of(wb_words, 0))
         for z in range(PASSES):
             nc.gpsimd.dma_start(out=xw[z][:], in_=words_of(xt_words, z))
-        nc.gpsimd.dma_start(out=bi_col[:], in_=bi.rearrange("o (p c) -> (o p) c", c=2))
-        nc.vector.memset(ident[:], 0.0)
-        make_identity(nc, ident[:], nomemset=True)
+        nc.gpsimd.dma_start(out=waw[:], in_=wa_words.rearrange("z p c t -> p z (c t)").bitcast(I32))
+        nc.gpsimd.dma_start(out=bias[:], in_=bi.to_broadcast([P, N]))
         for q in range(QUADS):
             scale_rows(nc.sync, xs, 0, xt_scales, q)
         for q in range(QUADS):
@@ -76,10 +74,7 @@ def tile_list_rows_owninput_gapoverpeak_kernel(
         for z in range(PASSES):
             nc.vector.tensor_copy(gs[:, z * J : (z + 1) * J], xs[:, z * T : (z + 1) * T].indirect(offsets[:]))
 
-        waw = sb.tile([P, PASSES, N], I32, name="waw", tag="xs_then_wa", align_bytes=64)
-        nc.sync.dma_start(out=waw[:], in_=wa_words.rearrange("z p c t -> p z (c t)").bitcast(I32))
-
-        sx_bf = sb.tile([P, J, PACK], BF16, name="sx_bf", align_bytes=64)
+        sx_bf = sb.tile([P, J, PACK], BF16, name="sx_bf", tag="sx_bf_then_gw1", align_bytes=64)
         nc.scalar.activation(
             out=sx_bf[:].rearrange("p (c i) t -> p c t i", i=4),
             in_=sx_raw[:].rearrange("p t (c i) -> p c t i", i=4),
@@ -90,19 +85,14 @@ def tile_list_rows_owninput_gapoverpeak_kernel(
         rs_raw = sb.tile([P, JT, N], F32, name="rs_raw", tag="sx_then_rs", align_bytes=64)
         nc.sync.dma_start(out=rs_raw[:], in_=rs.rearrange("(h p) n -> p h n", p=P))
 
-        bi_ps = ps.tile([P, 2, P], F32, name="bi_ps")
-        for c in range(2):
-            nc.tensor.transpose(bi_ps[:, c, :], bi_col[:, c : c + 1].to_broadcast([P, P]), ident[:])
-        bias = sb.tile([P, N], F32, name="bias")
-        nc.scalar.copy(out=bias[:].rearrange("q (p c) -> q p c", c=2), in_=bi_ps[:].rearrange("q c p -> q p c"))
-
-        gw = [sb.tile([P, J], U32, name="gw%d" % z, align_bytes=64) for z in range(PASSES)]
+        gw = [sb.tile([P, J], U32, name="gw0", align_bytes=64)]
         nc.vector.tensor_copy(gw[0][:], xw[0][:].bitcast(U32).indirect(offsets[:]))
 
         sq = sb.tile([P, J], U32, name="sq", align_bytes=64)
         sqs = sb.tile([P, J], U8, name="sqs", align_bytes=64)
         nc.vector.quantize_mx(out=sq[:].bitcast(E5M2), scales=sqs[:], in_=sx_bf[:].rearrange("p j t -> p (j t)"))
 
+        gw.append(sb.tile([P, J], U32, name="gw1", tag="sx_bf_then_gw1", align_bytes=64))
         nc.vector.tensor_copy(gw[1][:], xw[1][:].bitcast(U32).indirect(offsets[:]))
 
         rs3 = sb.tile([P, JT, N], F32, name="rs3")

@@ -1,6 +1,7 @@
 from contextlib import ExitStack
 
 import concourse.mybir as mybir
+from concourse.masks import make_identity
 
 K, T, J, N, L = 1024, 1024, 256, 256, 512
 FLOPS = 2 * J * N * (K + L)
@@ -39,7 +40,8 @@ def tile_list_rows_owninput_gapoverpeak_kernel(
         wbw = sb.tile([P, N], I32, name="wbw", align_bytes=64)
         sx_raw = sb.tile([P, PACK, J], F32, name="sx_raw", tag="sx_then_rs", align_bytes=64)
         waw = sb.tile([P, PASSES, N], I32, name="waw", align_bytes=64)
-        bias = sb.tile([P, N], F32, name="bias")
+        bi_col = sb.tile([P, 2], F32, name="bi_col")
+        ident = sb.tile([P, P], F32, name="ident", align_bytes=64)
 
         nc.vector.memset(xs[:].bitcast(I32), 0)
         nc.vector.memset(ws[:].bitcast(I32), 0)
@@ -57,12 +59,14 @@ def tile_list_rows_owninput_gapoverpeak_kernel(
             return src[z].rearrange("p c t -> p (c t)").bitcast(I32)
 
         nc.sync.dma_start(offsets[:], offs)
+        nc.sync.dma_start(out=bi_col[:], in_=bi.rearrange("o (p c) -> (o p) c", c=2))
         nc.scalar.dma_start(out=sx_raw[:], in_=sx.rearrange("(p t) j -> p t j", t=PACK))
         nc.scalar.dma_start(out=wbw[:], in_=words_of(wb_words, 0))
         for z in range(PASSES):
             nc.gpsimd.dma_start(out=xw[z][:], in_=words_of(xt_words, z))
         nc.gpsimd.dma_start(out=waw[:], in_=wa_words.rearrange("z p c t -> p z (c t)").bitcast(I32))
-        nc.gpsimd.dma_start(out=bias[:], in_=bi.to_broadcast([P, N]))
+        nc.vector.memset(ident[:], 0.0)
+        make_identity(nc, ident[:], nomemset=True)
         for q in range(QUADS):
             scale_rows(nc.sync, xs, 0, xt_scales, q)
         for q in range(QUADS):
@@ -85,6 +89,10 @@ def tile_list_rows_owninput_gapoverpeak_kernel(
         rs_raw = sb.tile([P, JT, N], F32, name="rs_raw", tag="sx_then_rs", align_bytes=64)
         nc.sync.dma_start(out=rs_raw[:], in_=rs.rearrange("(h p) n -> p h n", p=P))
 
+        bi_ps = ps.tile([P, 2, P], F32, name="bi_ps")
+        for c in range(2):
+            nc.tensor.transpose(bi_ps[:, c, :], bi_col[:, c : c + 1].to_broadcast([P, P]), ident[:])
+
         gw = [sb.tile([P, J], U32, name="gw0", align_bytes=64)]
         nc.vector.tensor_copy(gw[0][:], xw[0][:].bitcast(U32).indirect(offsets[:]))
 
@@ -94,6 +102,11 @@ def tile_list_rows_owninput_gapoverpeak_kernel(
 
         gw.append(sb.tile([P, J], U32, name="gw1", tag="sx_bf_then_gw1", align_bytes=64))
         nc.vector.tensor_copy(gw[1][:], xw[1][:].bitcast(U32).indirect(offsets[:]))
+
+        bias = sb.tile([P, N], F32, name="bias", tag="xw1", align_bytes=64)
+        nc.vector.tensor_copy(
+            out=bias[:].rearrange("q (p c) -> q p c", c=2), in_=bi_ps[:].rearrange("q c p -> q p c")
+        )
 
         rs3 = sb.tile([P, JT, N], F32, name="rs3")
         nc.scalar.activation(out=rs3[:], in_=rs_raw[:], func=ACT.Copy, scale=0.3)

@@ -45,6 +45,7 @@ def tile_list_rows_owninput_gapoverpeak_kernel(
 
         nc.vector.memset(xs[:].bitcast(I32), 0)
         nc.vector.memset(ws[:].bitcast(I32), 0)
+        nc.vector.memset(ident[:], 0.0)
 
         def scale_rows(queue, plane, first_word, src, q):
             passes = src.shape[0]
@@ -62,11 +63,10 @@ def tile_list_rows_owninput_gapoverpeak_kernel(
         nc.sync.dma_start(out=bi_col[:], in_=bi.rearrange("o (p c) -> (o p) c", c=2))
         nc.scalar.dma_start(out=sx_raw[:], in_=sx.rearrange("(p t) j -> p t j", t=PACK))
         nc.scalar.dma_start(out=wbw[:], in_=words_of(wb_words, 0))
-        for z in range(PASSES):
-            nc.gpsimd.dma_start(out=xw[z][:], in_=words_of(xt_words, z))
-        nc.gpsimd.dma_start(out=waw[:], in_=wa_words.rearrange("z p c t -> p z (c t)").bitcast(I32))
-        nc.vector.memset(ident[:], 0.0)
+        nc.gpsimd.dma_start(out=xw[0][:], in_=words_of(xt_words, 0))
         make_identity(nc, ident[:], nomemset=True)
+        nc.gpsimd.dma_start(out=waw[:], in_=wa_words.rearrange("z p c t -> p z (c t)").bitcast(I32))
+        nc.gpsimd.dma_start(out=xw[1][:], in_=words_of(xt_words, 1))
         for q in range(QUADS):
             scale_rows(nc.sync, xs, 0, xt_scales, q)
         for q in range(QUADS):
@@ -100,13 +100,16 @@ def tile_list_rows_owninput_gapoverpeak_kernel(
         sqs = sb.tile([P, J], U8, name="sqs", align_bytes=64)
         nc.vector.quantize_mx(out=sq[:].bitcast(E5M2), scales=sqs[:], in_=sx_bf[:].rearrange("p j t -> p (j t)"))
 
-        gw.append(sb.tile([P, J], U32, name="gw1", tag="sx_bf_then_gw1", align_bytes=64))
-        nc.vector.tensor_copy(gw[1][:], xw[1][:].bitcast(U32).indirect(offsets[:]))
-
-        bias = sb.tile([P, N], F32, name="bias", tag="xw1", align_bytes=64)
+        bias = sb.tile([P, N], F32, name="bias", tag="xw0", align_bytes=64)
         nc.vector.tensor_copy(
             out=bias[:].rearrange("q (p c) -> q p c", c=2), in_=bi_ps[:].rearrange("q c p -> q p c")
         )
+
+        gw.append(sb.tile([P, J], U32, name="gw1", tag="sx_bf_then_gw1", align_bytes=64))
+        for h in range(JT):
+            nc.vector.tensor_copy(
+                gw[1][:, h * P : (h + 1) * P], xw[1][:].bitcast(U32).indirect(offsets[:, h * 8 : (h + 1) * 8])
+            )
 
         rs3 = sb.tile([P, JT, N], F32, name="rs3")
         nc.scalar.activation(out=rs3[:], in_=rs_raw[:], func=ACT.Copy, scale=0.3)
@@ -137,25 +140,25 @@ def tile_list_rows_owninput_gapoverpeak_kernel(
                     stop=(step == 2),
                 )
 
-        for h in range(JT):
-            mx_pass(h, 0)
-        for h in range(JT):
-            mx_pass(h, 1)
-            mx_pass(h, 2)
+        for step in range(PASSES + 1):
+            for h in range(JT):
+                mx_pass(h, step)
 
+        d = [sb.tile([P, N], F32, name="d%d" % h) for h in range(JT)]
+        peak = sb.tile([P, JT], F32, name="peak")
+        den = sb.tile([P, JT], F32, name="den")
+        inv = sb.tile([P, JT], F32, name="inv")
+        y = [sb.tile([P, N], F32, name="y%d" % h) for h in range(JT)]
         for h in range(JT):
-            d = sb.tile([P, N], F32, name="d%d" % h)
-            peak = sb.tile([P, 1], F32, name="peak%d" % h)
-            den = sb.tile([P, 1], F32, name="den%d" % h)
-            inv = sb.tile([P, 1], F32, name="inv%d" % h)
-            y = sb.tile([P, N], F32, name="y%d" % h)
-            nc.vector.tensor_tensor(out=d[:], in0=acc[h][:], in1=bias[:], op=ALU.subtract)
+            nc.vector.tensor_tensor(out=d[h][:], in0=acc[h][:], in1=bias[:], op=ALU.subtract)
+        for h in range(JT):
             nc.vector.tensor_reduce(
-                out=peak[:], in_=d[:], axis=mybir.AxisListType.X, op=ALU.max, apply_absolute_value=True
+                out=peak[:, h : h + 1], in_=d[h][:], axis=mybir.AxisListType.X, op=ALU.max, apply_absolute_value=True
             )
-            nc.vector.tensor_scalar(out=den[:], in0=peak[:], scalar1=0.2, scalar2=None, op0=ALU.add)
-            nc.vector.reciprocal(out=inv[:], in_=den[:])
+        nc.vector.tensor_scalar(out=den[:], in0=peak[:], scalar1=0.2, scalar2=None, op0=ALU.add)
+        nc.vector.reciprocal(out=inv[:], in_=den[:])
+        for h in range(JT):
             nc.vector.scalar_tensor_tensor(
-                out=y[:], in0=d[:], scalar=inv[:], in1=rs3[:, h, :], op0=ALU.mult, op1=ALU.add
+                out=y[h][:], in0=d[h][:], scalar=inv[:, h : h + 1], in1=rs3[:, h, :], op0=ALU.mult, op1=ALU.add
             )
-            (nc.sync if h == 0 else nc.scalar).dma_start(out=out[h * P : (h + 1) * P, :], in_=y[:])
+            (nc.sync if h == 0 else nc.scalar).dma_start(out=out[h * P : (h + 1) * P, :], in_=y[h][:])

@@ -19,10 +19,13 @@ ACT = mybir.ActivationFunctionType
 
 P = 128
 PACK = 4
-PASSES = K // (P * PACK)
-QUADS = 4
-ROWS = 4
-JT = J // P
+XT_PASSES = K // (P * PACK)
+QUADRANT = 32
+SCALE_ROWS = 4
+SLOT_TILES = J // P
+LIST_GROUP = 16
+LINE = 4
+BIAS_PER_PARTITION = N // P
 
 
 def tile_list_rows_owninput_gapoverpeak_kernel(
@@ -33,132 +36,136 @@ def tile_list_rows_owninput_gapoverpeak_kernel(
         sb = ctx.enter_context(tc.tile_pool(name="sb", bufs=1))
         ps = ctx.enter_context(tc.psum_pool(name="ps", bufs=1))
 
-        offsets = sb.tile([P, J // 16], U16, name="offsets")
-        xs = sb.tile([P, PASSES * T], U8, name="xs", align_bytes=64)
-        ws = sb.tile([P, (PASSES + 1) * N], U8, name="ws", align_bytes=64)
-        xw = [sb.tile([P, T], I32, name="xw%d" % z, align_bytes=64) for z in range(PASSES)]
-        wbw = sb.tile([P, N], I32, name="wbw", align_bytes=64)
+        offsets = sb.tile([P, J // LIST_GROUP], U16, name="offsets")
+        xt_planes = sb.tile([P, XT_PASSES * T], U8, name="xt_planes", tag="planes_then_picked0", align_bytes=64)
+        w_planes = sb.tile([P, (XT_PASSES + 1) * N], U8, name="w_planes", align_bytes=64)
+        xt_sb = [sb.tile([P, T], I32, name="xt_sb%d" % z, align_bytes=64) for z in range(XT_PASSES)]
+        wb_sb = sb.tile([P, N], I32, name="wb_sb", align_bytes=64)
         sx_raw = sb.tile([P, PACK, J], F32, name="sx_raw", tag="sx_then_rs", align_bytes=64)
-        waw = sb.tile([P, PASSES, N], I32, name="waw", align_bytes=64)
-        bi_col = sb.tile([P, 2], F32, name="bi_col")
+        wa_sb = sb.tile([P, XT_PASSES, N], I32, name="wa_sb", align_bytes=64)
+        bi_col = sb.tile([P, BIAS_PER_PARTITION], F32, name="bi_col")
         ident = sb.tile([P, P], F32, name="ident", align_bytes=64)
 
-        nc.vector.memset(xs[:].bitcast(I32), 0)
-        nc.vector.memset(ws[:].bitcast(I32), 0)
+        nc.vector.memset(xt_planes[:].bitcast(I32), 0)
+        nc.vector.memset(w_planes[:].bitcast(I32), 0)
         nc.vector.memset(ident[:], 0.0)
 
-        def scale_rows(queue, plane, first_word, src, q):
-            passes = src.shape[0]
-            words = src.shape[2] // 4
-            dst = plane[32 * q : 32 * q + ROWS, :].bitcast(I32)[:, first_word : first_word + passes * words]
-            queue.dma_start(
-                out=dst.rearrange("r (z c) -> r z c", z=passes),
-                in_=src[:, ROWS * q : ROWS * (q + 1), :].bitcast(I32).rearrange("z r c -> r z c"),
-            )
+        def load_scale_rows(planes, first_byte, scales):
+            passes, width = scales.shape[0], scales.shape[2]
+            for q in range(P // QUADRANT):
+                rows = planes[QUADRANT * q : QUADRANT * q + SCALE_ROWS, :].bitcast(I32)
+                nc.sync.dma_start(
+                    out=rows[:, first_byte // 4 : (first_byte + passes * width) // 4].rearrange(
+                        "r (z c) -> r z c", z=passes
+                    ),
+                    in_=scales[:, SCALE_ROWS * q : SCALE_ROWS * (q + 1), :].bitcast(I32).rearrange("z r c -> r z c"),
+                )
 
-        def words_of(src, z):
-            return src[z].rearrange("p c t -> p (c t)").bitcast(I32)
+        def words_of_pass(words, z):
+            return words[z].rearrange("p c t -> p (c t)").bitcast(I32)
 
         nc.sync.dma_start(offsets[:], offs)
-        nc.sync.dma_start(out=bi_col[:], in_=bi.rearrange("o (p c) -> (o p) c", c=2))
+        nc.sync.dma_start(out=bi_col[:], in_=bi.rearrange("o (p c) -> (o p) c", c=BIAS_PER_PARTITION))
         nc.scalar.dma_start(out=sx_raw[:], in_=sx.rearrange("(p t) j -> p t j", t=PACK))
-        nc.scalar.dma_start(out=wbw[:], in_=words_of(wb_words, 0))
-        nc.gpsimd.dma_start(out=xw[0][:], in_=words_of(xt_words, 0))
+        nc.scalar.dma_start(out=wb_sb[:], in_=words_of_pass(wb_words, 0))
+        nc.gpsimd.dma_start(out=xt_sb[0][:], in_=words_of_pass(xt_words, 0))
         make_identity(nc, ident[:], nomemset=True)
-        nc.gpsimd.dma_start(out=waw[:], in_=wa_words.rearrange("z p c t -> p z (c t)").bitcast(I32))
-        nc.gpsimd.dma_start(out=xw[1][:], in_=words_of(xt_words, 1))
-        for q in range(QUADS):
-            scale_rows(nc.sync, xs, 0, xt_scales, q)
-        for q in range(QUADS):
-            scale_rows(nc.sync, ws, 0, wa_scales, q)
-        for q in range(QUADS):
-            scale_rows(nc.sync, ws, PASSES * N // 4, wb_scales, q)
+        nc.gpsimd.dma_start(out=wa_sb[:], in_=wa_words.rearrange("z p c t -> p z (c t)").bitcast(I32))
+        nc.gpsimd.dma_start(out=xt_sb[1][:], in_=words_of_pass(xt_words, 1))
+        load_scale_rows(xt_planes, 0, xt_scales)
+        load_scale_rows(w_planes, 0, wa_scales)
+        load_scale_rows(w_planes, XT_PASSES * N, wb_scales)
 
-        gs = sb.tile([P, PASSES * J], U8, name="gs", align_bytes=64)
-        for z in range(PASSES):
-            nc.vector.tensor_copy(gs[:, z * J : (z + 1) * J], xs[:, z * T : (z + 1) * T].indirect(offsets[:]))
+        picked_planes = sb.tile([P, XT_PASSES * J], U8, name="picked_planes", align_bytes=64)
+        for z in range(XT_PASSES):
+            nc.vector.tensor_copy(
+                picked_planes[:, z * J : (z + 1) * J], xt_planes[:, z * T : (z + 1) * T].indirect(offsets[:])
+            )
 
-        sx_bf = sb.tile([P, J, PACK], BF16, name="sx_bf", tag="sx_bf_then_gw1", align_bytes=64)
+        sx_bf = sb.tile([P, J, PACK], BF16, name="sx_bf", tag="sx_bf_then_picked1", align_bytes=64)
         nc.scalar.activation(
-            out=sx_bf[:].rearrange("p (c i) t -> p c t i", i=4),
-            in_=sx_raw[:].rearrange("p t (c i) -> p c t i", i=4),
+            out=sx_bf[:].rearrange("p (c i) t -> p c t i", i=LINE),
+            in_=sx_raw[:].rearrange("p t (c i) -> p c t i", i=LINE),
             func=ACT.Copy,
             scale=-1.0,
         )
 
-        rs_raw = sb.tile([P, JT, N], F32, name="rs_raw", tag="sx_then_rs", align_bytes=64)
+        rs_raw = sb.tile([P, SLOT_TILES, N], F32, name="rs_raw", tag="sx_then_rs", align_bytes=64)
         nc.sync.dma_start(out=rs_raw[:], in_=rs.rearrange("(h p) n -> p h n", p=P))
 
-        bi_ps = ps.tile([P, 2, P], F32, name="bi_ps")
-        for c in range(2):
-            nc.tensor.transpose(bi_ps[:, c, :], bi_col[:, c : c + 1].to_broadcast([P, P]), ident[:])
+        bias_ps = ps.tile([P, BIAS_PER_PARTITION, P], F32, name="bias_ps")
+        for c in range(BIAS_PER_PARTITION):
+            nc.tensor.transpose(bias_ps[:, c, :], bi_col[:, c : c + 1].to_broadcast([P, P]), ident[:])
 
-        gw = [sb.tile([P, J], U32, name="gw0", align_bytes=64)]
-        nc.vector.tensor_copy(gw[0][:], xw[0][:].bitcast(U32).indirect(offsets[:]))
+        picked0 = sb.tile([P, J], U32, name="picked0", tag="planes_then_picked0", align_bytes=64)
+        nc.vector.tensor_copy(picked0[:], xt_sb[0][:].bitcast(U32).indirect(offsets[:]))
 
-        sq = sb.tile([P, J], U32, name="sq", align_bytes=64)
-        sqs = sb.tile([P, J], U8, name="sqs", align_bytes=64)
-        nc.vector.quantize_mx(out=sq[:].bitcast(E5M2), scales=sqs[:], in_=sx_bf[:].rearrange("p j t -> p (j t)"))
-
-        bias = sb.tile([P, N], F32, name="bias", tag="xw0", align_bytes=64)
-        nc.vector.tensor_copy(
-            out=bias[:].rearrange("q (p c) -> q p c", c=2), in_=bi_ps[:].rearrange("q c p -> q p c")
+        sx_codes = sb.tile([P, J], U32, name="sx_codes", align_bytes=64)
+        sx_plane = sb.tile([P, J], U8, name="sx_plane", align_bytes=64)
+        nc.vector.quantize_mx(
+            out=sx_codes[:].bitcast(E5M2), scales=sx_plane[:], in_=sx_bf[:].rearrange("p j t -> p (j t)")
         )
 
-        gw.append(sb.tile([P, J], U32, name="gw1", tag="sx_bf_then_gw1", align_bytes=64))
-        for h in range(JT):
+        bias = sb.tile([P, N], F32, name="bias", tag="xt_sb0", align_bytes=64)
+        nc.vector.tensor_copy(
+            out=bias[:].rearrange("q (p c) -> q p c", c=BIAS_PER_PARTITION),
+            in_=bias_ps[:].rearrange("q c p -> q p c"),
+        )
+
+        picked1 = sb.tile([P, J], U32, name="picked1", tag="sx_bf_then_picked1", align_bytes=64)
+        list_cols = P // LIST_GROUP
+        for h in range(SLOT_TILES):
             nc.vector.tensor_copy(
-                gw[1][:, h * P : (h + 1) * P], xw[1][:].bitcast(U32).indirect(offsets[:, h * 8 : (h + 1) * 8])
+                picked1[:, h * P : (h + 1) * P],
+                xt_sb[1][:].bitcast(U32).indirect(offsets[:, h * list_cols : (h + 1) * list_cols]),
             )
 
-        rs3 = sb.tile([P, JT, N], F32, name="rs3")
-        nc.scalar.activation(out=rs3[:], in_=rs_raw[:], func=ACT.Copy, scale=0.3)
+        rs_scaled = sb.tile([P, SLOT_TILES, N], F32, name="rs_scaled")
+        nc.scalar.activation(out=rs_scaled[:], in_=rs_raw[:], func=ACT.Copy, scale=0.3)
 
-        acc = [ps.tile([P, N], F32, name="acc%d" % h) for h in range(JT)]
-
-        def mx_pass(h, step):
-            cols = slice(h * P, (h + 1) * P)
-            if step == 0:
+        acc = [ps.tile([P, N], F32, name="acc%d" % h) for h in range(SLOT_TILES)]
+        passes = [
+            (picked0[:].bitcast(E4M3), picked_planes[:, 0:J], wa_sb[:, 0, :], w_planes[:, 0:N]),
+            (sx_codes[:].bitcast(E5M2), sx_plane[:], wb_sb[:], w_planes[:, XT_PASSES * N :]),
+            (picked1[:].bitcast(E4M3), picked_planes[:, J:], wa_sb[:, 1, :], w_planes[:, N : XT_PASSES * N]),
+        ]
+        for step, (slot_codes, slot_plane, weight_words, weight_plane) in enumerate(passes):
+            for h in range(SLOT_TILES):
                 nc.tensor.matmul_mx(
                     out=acc[h][:],
-                    lhsT=sq[:, cols].bitcast(E5M2),
-                    lhsT_scale=sqs[:, cols],
-                    rhs=wbw[:].bitcast(E5M2),
-                    rhs_scale=ws[:, PASSES * N : (PASSES + 1) * N],
-                    start=True,
-                    stop=False,
-                )
-            else:
-                z = step - 1
-                nc.tensor.matmul_mx(
-                    out=acc[h][:],
-                    lhsT=gw[z][:, cols].bitcast(E4M3),
-                    lhsT_scale=gs[:, z * J + h * P : z * J + (h + 1) * P],
-                    rhs=waw[:, z, :].bitcast(E5M2),
-                    rhs_scale=ws[:, z * N : (z + 1) * N],
-                    start=False,
-                    stop=(step == 2),
+                    lhsT=slot_codes[:, h * P : (h + 1) * P],
+                    lhsT_scale=slot_plane[:, h * P : (h + 1) * P],
+                    rhs=weight_words.bitcast(E5M2),
+                    rhs_scale=weight_plane,
+                    start=(step == 0),
+                    stop=(step == len(passes) - 1),
                 )
 
-        for step in range(PASSES + 1):
-            for h in range(JT):
-                mx_pass(h, step)
-
-        d = [sb.tile([P, N], F32, name="d%d" % h) for h in range(JT)]
-        peak = sb.tile([P, JT], F32, name="peak")
-        den = sb.tile([P, JT], F32, name="den")
-        inv = sb.tile([P, JT], F32, name="inv")
-        y = [sb.tile([P, N], F32, name="y%d" % h) for h in range(JT)]
-        for h in range(JT):
-            nc.vector.tensor_tensor(out=d[h][:], in0=acc[h][:], in1=bias[:], op=ALU.subtract)
-        for h in range(JT):
+        gap = [sb.tile([P, N], F32, name="gap%d" % h) for h in range(SLOT_TILES)]
+        peak = sb.tile([P, SLOT_TILES], F32, name="peak")
+        divisor = sb.tile([P, SLOT_TILES], F32, name="divisor")
+        inverse = sb.tile([P, SLOT_TILES], F32, name="inverse")
+        result = [sb.tile([P, N], F32, name="result%d" % h) for h in range(SLOT_TILES)]
+        for h in range(SLOT_TILES):
+            nc.vector.tensor_tensor(out=gap[h][:], in0=acc[h][:], in1=bias[:], op=ALU.subtract)
+        for h in range(SLOT_TILES):
             nc.vector.tensor_reduce(
-                out=peak[:, h : h + 1], in_=d[h][:], axis=mybir.AxisListType.X, op=ALU.max, apply_absolute_value=True
+                out=peak[:, h : h + 1],
+                in_=gap[h][:],
+                axis=mybir.AxisListType.X,
+                op=ALU.max,
+                apply_absolute_value=True,
             )
-        nc.vector.tensor_scalar(out=den[:], in0=peak[:], scalar1=0.2, scalar2=None, op0=ALU.add)
-        nc.vector.reciprocal(out=inv[:], in_=den[:])
-        for h in range(JT):
+        nc.vector.tensor_scalar(out=divisor[:], in0=peak[:], scalar1=0.2, scalar2=None, op0=ALU.add)
+        nc.vector.reciprocal(out=inverse[:], in_=divisor[:])
+        store_queues = [nc.sync, nc.scalar]
+        for h in range(SLOT_TILES):
             nc.vector.scalar_tensor_tensor(
-                out=y[h][:], in0=d[h][:], scalar=inv[:, h : h + 1], in1=rs3[:, h, :], op0=ALU.mult, op1=ALU.add
+                out=result[h][:],
+                in0=gap[h][:],
+                scalar=inverse[:, h : h + 1],
+                in1=rs_scaled[:, h, :],
+                op0=ALU.mult,
+                op1=ALU.add,
             )
-            (nc.sync if h == 0 else nc.scalar).dma_start(out=out[h * P : (h + 1) * P, :], in_=y[h][:])
+            store_queues[h].dma_start(out=out[h * P : (h + 1) * P, :], in_=result[h][:])

from contextlib import ExitStack

import concourse.mybir as mybir
from concourse.masks import make_identity

K, T, J, N, L = 1024, 1024, 256, 256, 512
FLOPS = 2 * J * N * (K + L)

F32 = mybir.dt.float32
BF16 = mybir.dt.bfloat16
I32 = mybir.dt.int32
U32 = mybir.dt.uint32
U16 = mybir.dt.uint16
U8 = mybir.dt.uint8
E4M3 = mybir.dt.float8_e4m3fn_x4
E5M2 = mybir.dt.float8_e5m2_x4
ALU = mybir.AluOpType
ACT = mybir.ActivationFunctionType

P = 128
PACK = 4
XT_PASSES = K // (P * PACK)
QUADRANT = 32
SCALE_ROWS = 4
SLOT_TILES = J // P
LIST_GROUP = 16
LINE = 4
BIAS_PER_PARTITION = N // P


def tile_list_rows_owninput_gapoverpeak_kernel(
    tc, xt_words, xt_scales, wa_words, wa_scales, sx, wb_words, wb_scales, bi, rs, offs, out
):
    nc = tc.nc
    with ExitStack() as ctx:
        sb = ctx.enter_context(tc.tile_pool(name="sb", bufs=1))
        ps = ctx.enter_context(tc.psum_pool(name="ps", bufs=1))

        offsets = sb.tile([P, J // LIST_GROUP], U16, name="offsets")
        xt_planes = sb.tile([P, XT_PASSES * T], U8, name="xt_planes", tag="planes_then_picked0", align_bytes=64)
        w_planes = sb.tile([P, (XT_PASSES + 1) * N], U8, name="w_planes", align_bytes=64)
        xt_sb = [sb.tile([P, T], I32, name="xt_sb%d" % z, align_bytes=64) for z in range(XT_PASSES)]
        wb_sb = sb.tile([P, N], I32, name="wb_sb", align_bytes=64)
        sx_raw = sb.tile([P, PACK, J], F32, name="sx_raw", tag="sx_then_rs", align_bytes=64)
        wa_sb = sb.tile([P, XT_PASSES, N], I32, name="wa_sb", align_bytes=64)
        bi_col = sb.tile([P, BIAS_PER_PARTITION], F32, name="bi_col")
        ident = sb.tile([P, P], F32, name="ident", align_bytes=64)

        nc.vector.memset(xt_planes[:].bitcast(I32), 0)
        nc.vector.memset(w_planes[:].bitcast(I32), 0)
        nc.vector.memset(ident[:], 0.0)

        def load_scale_rows(planes, first_byte, scales):
            passes, width = scales.shape[0], scales.shape[2]
            for q in range(P // QUADRANT):
                rows = planes[QUADRANT * q : QUADRANT * q + SCALE_ROWS, :].bitcast(I32)
                nc.sync.dma_start(
                    out=rows[:, first_byte // 4 : (first_byte + passes * width) // 4].rearrange(
                        "r (z c) -> r z c", z=passes
                    ),
                    in_=scales[:, SCALE_ROWS * q : SCALE_ROWS * (q + 1), :].bitcast(I32).rearrange("z r c -> r z c"),
                )

        def words_of_pass(words, z):
            return words[z].rearrange("p c t -> p (c t)").bitcast(I32)

        nc.sync.dma_start(offsets[:], offs)
        nc.sync.dma_start(out=bi_col[:], in_=bi.rearrange("o (p c) -> (o p) c", c=BIAS_PER_PARTITION))
        nc.scalar.dma_start(out=sx_raw[:], in_=sx.rearrange("(p t) j -> p t j", t=PACK))
        nc.scalar.dma_start(out=wb_sb[:], in_=words_of_pass(wb_words, 0))
        nc.gpsimd.dma_start(out=xt_sb[0][:], in_=words_of_pass(xt_words, 0))
        make_identity(nc, ident[:], nomemset=True)
        nc.gpsimd.dma_start(out=wa_sb[:], in_=wa_words.rearrange("z p c t -> p z (c t)").bitcast(I32))
        nc.gpsimd.dma_start(out=xt_sb[1][:], in_=words_of_pass(xt_words, 1))
        load_scale_rows(xt_planes, 0, xt_scales)
        load_scale_rows(w_planes, 0, wa_scales)
        load_scale_rows(w_planes, XT_PASSES * N, wb_scales)

        picked_planes = sb.tile([P, XT_PASSES * J], U8, name="picked_planes", align_bytes=64)
        for z in range(XT_PASSES):
            nc.vector.tensor_copy(
                picked_planes[:, z * J : (z + 1) * J], xt_planes[:, z * T : (z + 1) * T].indirect(offsets[:])
            )

        sx_bf = sb.tile([P, J, PACK], BF16, name="sx_bf", tag="sx_bf_then_picked1", align_bytes=64)
        nc.scalar.activation(
            out=sx_bf[:].rearrange("p (c i) t -> p c t i", i=LINE),
            in_=sx_raw[:].rearrange("p t (c i) -> p c t i", i=LINE),
            func=ACT.Copy,
            scale=-1.0,
        )

        rs_raw = sb.tile([P, SLOT_TILES, N], F32, name="rs_raw", tag="sx_then_rs", align_bytes=64)
        nc.sync.dma_start(out=rs_raw[:], in_=rs.rearrange("(h p) n -> p h n", p=P))

        bias_ps = ps.tile([P, BIAS_PER_PARTITION, P], F32, name="bias_ps")
        for c in range(BIAS_PER_PARTITION):
            nc.tensor.transpose(bias_ps[:, c, :], bi_col[:, c : c + 1].to_broadcast([P, P]), ident[:])

        picked0 = sb.tile([P, J], U32, name="picked0", tag="planes_then_picked0", align_bytes=64)
        nc.vector.tensor_copy(picked0[:], xt_sb[0][:].bitcast(U32).indirect(offsets[:]))

        sx_codes = sb.tile([P, J], U32, name="sx_codes", align_bytes=64)
        sx_plane = sb.tile([P, J], U8, name="sx_plane", align_bytes=64)
        nc.vector.quantize_mx(
            out=sx_codes[:].bitcast(E5M2), scales=sx_plane[:], in_=sx_bf[:].rearrange("p j t -> p (j t)")
        )

        bias = sb.tile([P, N], F32, name="bias", tag="xt_sb0", align_bytes=64)
        nc.vector.tensor_copy(
            out=bias[:].rearrange("q (p c) -> q p c", c=BIAS_PER_PARTITION),
            in_=bias_ps[:].rearrange("q c p -> q p c"),
        )

        picked1 = sb.tile([P, J], U32, name="picked1", tag="sx_bf_then_picked1", align_bytes=64)
        list_cols = P // LIST_GROUP
        for h in range(SLOT_TILES):
            nc.vector.tensor_copy(
                picked1[:, h * P : (h + 1) * P],
                xt_sb[1][:].bitcast(U32).indirect(offsets[:, h * list_cols : (h + 1) * list_cols]),
            )

        rs_scaled = sb.tile([P, SLOT_TILES, N], F32, name="rs_scaled")
        nc.scalar.activation(out=rs_scaled[:], in_=rs_raw[:], func=ACT.Copy, scale=0.3)

        acc = [ps.tile([P, N], F32, name="acc%d" % h) for h in range(SLOT_TILES)]
        passes = [
            (picked0[:].bitcast(E4M3), picked_planes[:, 0:J], wa_sb[:, 0, :], w_planes[:, 0:N]),
            (sx_codes[:].bitcast(E5M2), sx_plane[:], wb_sb[:], w_planes[:, XT_PASSES * N :]),
            (picked1[:].bitcast(E4M3), picked_planes[:, J:], wa_sb[:, 1, :], w_planes[:, N : XT_PASSES * N]),
        ]
        for step, (slot_codes, slot_plane, weight_words, weight_plane) in enumerate(passes):
            for h in range(SLOT_TILES):
                nc.tensor.matmul_mx(
                    out=acc[h][:],
                    lhsT=slot_codes[:, h * P : (h + 1) * P],
                    lhsT_scale=slot_plane[:, h * P : (h + 1) * P],
                    rhs=weight_words.bitcast(E5M2),
                    rhs_scale=weight_plane,
                    start=(step == 0),
                    stop=(step == len(passes) - 1),
                )

        gap = [sb.tile([P, N], F32, name="gap%d" % h) for h in range(SLOT_TILES)]
        peak = sb.tile([P, SLOT_TILES], F32, name="peak")
        divisor = sb.tile([P, SLOT_TILES], F32, name="divisor")
        inverse = sb.tile([P, SLOT_TILES], F32, name="inverse")
        result = [sb.tile([P, N], F32, name="result%d" % h) for h in range(SLOT_TILES)]
        for h in range(SLOT_TILES):
            nc.vector.tensor_tensor(out=gap[h][:], in0=acc[h][:], in1=bias[:], op=ALU.subtract)
        for h in range(SLOT_TILES):
            nc.vector.tensor_reduce(
                out=peak[:, h : h + 1],
                in_=gap[h][:],
                axis=mybir.AxisListType.X,
                op=ALU.max,
                apply_absolute_value=True,
            )
        nc.vector.tensor_scalar(out=divisor[:], in0=peak[:], scalar1=0.2, scalar2=None, op0=ALU.add)
        nc.vector.reciprocal(out=inverse[:], in_=divisor[:])
        store_queues = [nc.sync, nc.scalar]
        for h in range(SLOT_TILES):
            nc.vector.scalar_tensor_tensor(
                out=result[h][:],
                in0=gap[h][:],
                scalar=inverse[:, h : h + 1],
                in1=rs_scaled[:, h, :],
                op0=ALU.mult,
                op1=ALU.add,
            )
            store_queues[h].dma_start(out=out[h * P : (h + 1) * P, :], in_=result[h][:])
